import numpy as np
import ml_dtypes


def mxq(x, axis, fmt="e4m3"):
    dtype, down = {"e4m3": (ml_dtypes.float8_e4m3fn, 7), "e5m2": (ml_dtypes.float8_e5m2, 14)}[fmt]
    v = np.moveaxis(np.asarray(x, np.float32).astype(ml_dtypes.bfloat16).astype(np.float64), axis, -1)
    blocks = v.reshape(v.shape[:-1] + (-1, 32))
    amax = np.abs(blocks).max(-1, keepdims=True)
    byte = np.maximum(np.where(amax > 0, np.frexp(amax)[1] - 1 + 127, 0) - down, 1)
    scale = np.exp2(byte - 127.0)
    codes = (blocks / scale).astype(np.float32).astype(dtype).astype(np.float64)
    return np.moveaxis((codes * scale).reshape(v.shape), -1, axis)


WIDE = False


def mx_kscale(k):
    if not WIDE:
        return np.ones(k)
    levels = np.array([10, -10, 5, -5, 0])
    if k % 512:
        return np.exp2(np.random.permutation(np.resize(levels, k // 32))).repeat(32)
    a = np.empty((k // 512, 16))
    for p in range(k // 512):
        a[p, :8] = np.random.permutation(np.resize(levels, 8))
        for g in range(8):
            far = levels[np.abs(levels - a[p, g]) >= 10]
            a[p, g + 8] = far[np.random.randint(len(far))]
    return np.exp2(a.ravel()).repeat(32)


def f64(x):
    return np.asarray(x).astype(np.float64)


def striped(idx):
    return np.tile(idx.reshape(-1, 16).T, (8, 1)).astype(np.uint16)


def unstriped(offs):
    return offs[:16].T.reshape(-1).astype(np.int64)


def pack_weight(w):
    k, n = w.shape
    w = f64(np.asarray(w, np.float32).astype(ml_dtypes.bfloat16)).reshape(k // 32, 32, n)
    amax = np.abs(w).max(1)
    byte = np.clip(np.where(amax > 0, np.frexp(amax)[1] - 1 + 127 - 7, 1), 1, 254)
    scaled = (w * np.exp2(127.0 - byte)[:, None, :]).reshape(k, n).astype(np.float32)
    words = np.ascontiguousarray(scaled.reshape(k // 512, 128, 4, n).transpose(0, 1, 3, 2)).astype(ml_dtypes.float8_e4m3fn).view(np.uint8)
    return words, np.ascontiguousarray(byte.astype(np.uint8).reshape(k // 512, 16, n))


def unpack_weight(words, scales):
    g, p, n, _ = words.shape
    vals = np.ascontiguousarray(words).view(ml_dtypes.float8_e4m3fn).astype(np.float64) * np.repeat(np.exp2(scales.astype(np.float64) - 127.0), 8, axis=1)[..., None]
    return vals.transpose(0, 1, 3, 2).reshape(g * 512, n)


K, T, S, N, H, U = 1024, 2048, 512, 128, 512, 1024


def setup_inputs():
    n = np.random.standard_normal
    s = mx_kscale(K)[:, None]
    u = mx_kscale(H)
    packed_xT = pack_weight(n((K, T)) * s)
    return {
        "x_words": packed_xT[0],
        "x_scales": packed_xT[1],
        "w1": (n((K, H)) / np.sqrt(K) / s).astype(np.float32),
        "unit": (np.random.uniform(0.6, 1.4, (H, 1)) * u[:, None]).astype(np.float32),
        "w2": (n((H, N)) / np.sqrt(H) / u[:, None]).astype(np.float32),
        "offs": striped(np.random.permutation(T)[:S]),
        "mot": striped(np.random.permutation(np.concatenate([np.arange(S), np.random.randint(0, S, U - S)]))),
        "fat": striped(np.random.permutation(np.concatenate([np.arange(S), np.random.randint(0, S, U - S)]))),
        "kid": striped(np.random.permutation(np.concatenate([np.arange(S), np.random.randint(0, S, U - S)]))),
    }


def reference(x_words, x_scales, w1, unit, w2, offs, mot, fat, kid):
    xq = unpack_weight(x_words, x_scales)[:, unstriped(offs)]
    y = mxq(f64(w1), 0, "e4m3").T @ xq
    ym = y[:, unstriped(mot)]
    yf = y[:, unstriped(fat)]
    mid = ym + yf
    yk = y[:, unstriped(kid)]
    hid = f64(unit) * (mid * yk)
    return mxq(f64(w2), 0, "e4m3").T @ mxq(hid, 0, "e4m3")

@@ -1,0 +1,191 @@
+from contextlib import ExitStack
+
+import concourse.mybir as mybir
+
+F32 = mybir.dt.float32
+BF16 = mybir.dt.bfloat16
+I32 = mybir.dt.int32
+U32 = mybir.dt.uint32
+U16 = mybir.dt.uint16
+U8 = mybir.dt.uint8
+FP8X4 = mybir.dt.float8_e4m3fn_x4
+ADD = mybir.AluOpType.add
+MULT = mybir.AluOpType.mult
+COPY = mybir.ActivationFunctionType.Copy
+
+P = 128
+K, T, S, H, N, U = 1024, 2048, 512, 512, 128, 1024
+FLOPS = 2 * K * H * S + 2 * H * N * U
+CHUNKS = [(256, True), (256, False), (256, False), (128, False), (128, False)]
+
+
+def tile_picked_ytenrel_mul_p_kernel(tc, x_words, x_scales, w1, unit, w2, offs, mot, fat, kid, out):
+    nc = tc.nc
+    with ExitStack() as ctx:
+        keep = ctx.enter_context(tc.tile_pool(name="keep", bufs=1))
+        psum = ctx.enter_context(tc.psum_pool(name="psum", bufs=1))
+        psum_out = ctx.enter_context(tc.psum_pool(name="psum_out", bufs=2))
+
+        offs_t = keep.tile([P, S // 16], U16, name="offs_t")
+        mot_t = keep.tile([P, U // 16], U16, name="mot_t")
+        fat_t = keep.tile([P, U // 16], U16, name="fat_t")
+        kid_t = keep.tile([P, U // 16], U16, name="kid_t")
+        xw = [keep.tile([P, T], I32, name=f"xw{o}", align_bytes=64) for o in range(2)]
+        xs = keep.tile([P, T], U8, name="xs", align_bytes=64)
+        w1_raw = [keep.tile([P, 4, H], F32, name=f"w1_raw{o}", align_bytes=64) for o in range(2)]
+        w2_raw = keep.tile([P, 4, N], F32, name="w2_raw", align_bytes=64)
+        unit_t = keep.tile([P, 4], F32, name="unit_t")
+        y = [keep.tile([P, S], F32, name=f"y{t}", align_bytes=64) for t in range(4)]
+        uy = [keep.tile([P, S], F32, name=f"uy{t}", align_bytes=64) for t in range(4)]
+
+        nc.vector.memset(xs[:].bitcast(I32), 0)
+
+        def load_w1(o):
+            nc.sync.dma_start(out=w1_raw[o][:], in_=w1[512 * o : 512 * (o + 1), :].rearrange("(p j) c -> p j c", j=4))
+
+        def load_x(o):
+            nc.sync.dma_start(out=xw[o][:], in_=x_words[o].rearrange("p n r -> p (n r)").bitcast(I32))
+
+        nc.sync.dma_start(offs_t[:], offs)
+        load_w1(0)
+        load_x(0)
+        for q in range(4):
+            nc.sync.dma_start(out=xs[32 * q : 32 * q + 8, :].bitcast(I32), in_=x_scales[:, 4 * q : 4 * q + 4, :].bitcast(I32))
+        load_w1(1)
+        load_x(1)
+        nc.sync.dma_start(mot_t[:], mot)
+        nc.sync.dma_start(fat_t[:], fat)
+        nc.sync.dma_start(kid_t[:], kid)
+        nc.sync.dma_start(out=unit_t[:], in_=unit.rearrange("(p t) o -> p (t o)", t=4))
+        nc.sync.dma_start(out=w2_raw[:], in_=w2.rearrange("(p j) n -> p j n", j=4))
+
+        gw = [keep.tile([P, S], U32, name=f"gw{o}", align_bytes=64) for o in range(2)]
+        gs = keep.tile([P, S], U8, name="gs", align_bytes=64)
+        w1_bf = [keep.tile([P, 4 * H], BF16, name=f"w1_bf{o}", align_bytes=64) for o in range(2)]
+        w1_c = [keep.tile([P, H], U32, name=f"w1_c{o}", align_bytes=64) for o in range(2)]
+        w1_s = [keep.tile([P, H], U8, name=f"w1_s{o}", align_bytes=64) for o in range(2)]
+        banks = [psum.tile([P, S], F32, name=f"bank{t}") for t in range(4)]
+
+        def cast_w1(o, copy, m0, m1):
+            dst = w1_bf[o][:].rearrange("p (t m j) -> p m j t", t=4, j=4)[:, m0:m1]
+            src = w1_raw[o][:].rearrange("p j (m t) -> p m j t", t=4)[:, m0:m1]
+            copy(dst, src)
+
+        def quantize_w1(o):
+            nc.vector.quantize_mx(out=w1_c[o][:].bitcast(FP8X4), scales=w1_s[o][:], in_=w1_bf[o][:])
+
+        def gather_x(o):
+            nc.vector.tensor_copy(gw[o][:], xw[o][:].bitcast(U32).indirect(offs_t[:]))
+
+        def first_product(o):
+            for t in range(4):
+                cols = slice(P * t, P * (t + 1))
+                nc.tensor.matmul_mx(
+                    out=banks[t][:],
+                    lhsT=w1_c[o][:, cols].bitcast(FP8X4),
+                    lhsT_scale=w1_s[o][:, cols],
+                    rhs=gw[o][:].bitcast(FP8X4),
+                    rhs_scale=gs[4 * o : P, :],
+                    start=(o == 0),
+                    stop=(o == 1),
+                )
+
+        cast_w1(0, nc.scalar.copy, 0, 128)
+        nc.vector.tensor_copy(gs[:], xs[:].indirect(offs_t[:]))
+        gather_x(0)
+        quantize_w1(0)
+        first_product(0)
+        cast_w1(1, nc.scalar.copy, 0, 48)
+        cast_w1(1, nc.vector.tensor_copy, 48, 128)
+        quantize_w1(1)
+        gather_x(1)
+        first_product(1)
+
+        w2_bf = keep.tile([P, 4 * N], BF16, name="w2_bf", align_bytes=64)
+        w2_c = keep.tile([P, N], U32, name="w2_c", align_bytes=64)
+        w2_s = keep.tile([P, N], U8, name="w2_s", align_bytes=64)
+
+        nc.scalar.copy(w2_bf[:].rearrange("p (c i j) -> p c j i", i=4, j=4), w2_raw[:].rearrange("p j (c i) -> p c j i", i=4))
+        nc.vector.quantize_mx(out=w2_c[:].bitcast(FP8X4), scales=w2_s[:], in_=w2_bf[:])
+
+        starts = [sum(w for w, fused in CHUNKS[:c]) for c in range(len(CHUNKS))]
+
+        def offsets(list_tile, c):
+            return list_tile[:, starts[c] // 16 : (starts[c] + CHUNKS[c][0]) // 16]
+
+        mother = [[keep.tile([P, w], F32, name=f"mother{c}_{t}", align_bytes=64) for t in range(4)] for c, (w, fused) in enumerate(CHUNKS)]
+        mid = [keep.tile([P, 4, w], F32, name=f"mid{c}", align_bytes=64) for c, (w, fused) in enumerate(CHUNKS)]
+        other = [keep.tile([P, 4, w], F32, name=f"other{c}", align_bytes=64) for c, (w, fused) in enumerate(CHUNKS)]
+        hid = [keep.tile([P, 4 * w], BF16, name=f"hid{c}", align_bytes=64) for c, (w, fused) in enumerate(CHUNKS)]
+        hid_c = [keep.tile([P, w], U32, name=f"hid_c{c}", align_bytes=64) for c, (w, fused) in enumerate(CHUNKS)]
+        hid_s = [keep.tile([P, w], U8, name=f"hid_s{c}", align_bytes=64) for c, (w, fused) in enumerate(CHUNKS)]
+        res = [keep.tile([P, w], F32, name=f"res{c}", align_bytes=64) for c, (w, fused) in enumerate(CHUNKS)]
+
+        def leave_bank(t):
+            if t == 1:
+                nc.vector.tensor_copy(y[t][:], banks[t][:])
+            else:
+                nc.scalar.copy(y[t][:], banks[t][:])
+
+        def scale_table(t):
+            nc.vector.tensor_scalar_mul(uy[t][:], y[t][:], unit_t[:, t : t + 1])
+
+        def gather_mother(c, t):
+            nc.scalar.activation(mother[c][t][:], y[t][:].indirect(offsets(mot_t, c)), COPY)
+
+        def add_father(c, t):
+            nc.vector.tensor_tensor(mid[c][:, t, :], y[t][:].indirect(offsets(fat_t, c)), mother[c][t][:], ADD)
+
+        def gather_kid(c, t):
+            nc.scalar.activation(other[c][:, t, :], uy[t][:].indirect(offsets(kid_t, c)), COPY)
+
+        def times_kid(c, t):
+            nc.vector.tensor_tensor(other[c][:, t, :], uy[t][:].indirect(offsets(kid_t, c)), mid[c][:, t, :], MULT)
+
+        def weave(c):
+            dst = hid[c][:].rearrange("p (g i t) -> p g t i", i=4, t=4)
+            a = other[c][:].rearrange("p t (g i) -> p g t i", i=4)
+            if CHUNKS[c][1]:
+                nc.vector.tensor_copy(dst, a)
+            else:
+                nc.vector.tensor_tensor(dst, a, mid[c][:].rearrange("p t (g i) -> p g t i", i=4), MULT)
+
+        def quantize_hid(c):
+            nc.vector.quantize_mx(out=hid_c[c][:].bitcast(FP8X4), scales=hid_s[c][:], in_=hid[c][:])
+
+        def second_product(c):
+            w = CHUNKS[c][0]
+            acc = psum_out.tile([P, 512], F32, name="acc")
+            nc.tensor.matmul_mx(
+                out=acc[:, :w],
+                lhsT=w2_c[:].bitcast(FP8X4),
+                lhsT_scale=w2_s[:],
+                rhs=hid_c[c][:].bitcast(FP8X4),
+                rhs_scale=hid_s[c][:],
+                start=True,
+                stop=True,
+            )
+            nc.scalar.copy(res[c][:], acc[:, :w])
+            nc.sync.dma_start(out=out[:, starts[c] : starts[c] + w], in_=res[c][:])
+
+        for t in range(4):
+            leave_bank(t)
+            gather_mother(0, t)
+            scale_table(t)
+            add_father(0, t)
+        last = len(CHUNKS) - 1
+        for c in range(len(CHUNKS)):
+            for t in range(4):
+                if c < last:
+                    gather_mother(c + 1, t)
+                if CHUNKS[c][1]:
+                    times_kid(c, t)
+                else:
+                    gather_kid(c, t)
+                if c < last and t < 3:
+                    add_father(c + 1, t)
+            weave(c)
+            if c < last:
+                add_father(c + 1, 3)
+            quantize_hid(c)
+            second_product(c)

@@ -16,7 +16,8 @@ COPY = mybir.ActivationFunctionType.Copy
 P = 128
 K, T, S, H, N, U = 1024, 2048, 512, 512, 128, 1024
 FLOPS = 2 * K * H * S + 2 * H * N * U
-CHUNKS = [(256, True), (256, False), (256, False), (128, False), (128, False)]
+CHUNKS = [(256, True), (384, False), (256, False), (128, False)]
+SCALAR_CAST = (64, 32)
 
 
 def tile_picked_ytenrel_mul_p_kernel(tc, x_words, x_scales, w1, unit, w2, offs, mot, fat, kid, out):
@@ -24,13 +25,13 @@ def tile_picked_ytenrel_mul_p_kernel(tc, x_words, x_scales, w1, unit, w2, offs, 
     with ExitStack() as ctx:
         keep = ctx.enter_context(tc.tile_pool(name="keep", bufs=1))
         psum = ctx.enter_context(tc.psum_pool(name="psum", bufs=1))
-        psum_out = ctx.enter_context(tc.psum_pool(name="psum_out", bufs=2))
+        psum_out = ctx.enter_context(tc.psum_pool(name="psum_out", bufs=4))
 
         offs_t = keep.tile([P, S // 16], U16, name="offs_t")
         mot_t = keep.tile([P, U // 16], U16, name="mot_t")
         fat_t = keep.tile([P, U // 16], U16, name="fat_t")
         kid_t = keep.tile([P, U // 16], U16, name="kid_t")
-        xw = [keep.tile([P, T], I32, name=f"xw{o}", align_bytes=64) for o in range(2)]
+        xw = [keep.tile([P, T], I32, name=f"xw{o}", tag=f"xw{o}", align_bytes=64) for o in range(2)]
         xs = keep.tile([P, T], U8, name="xs", align_bytes=64)
         w1_raw = [keep.tile([P, 4, H], F32, name=f"w1_raw{o}", align_bytes=64) for o in range(2)]
         w2_raw = keep.tile([P, 4, N], F32, name="w2_raw", align_bytes=64)
@@ -38,73 +39,76 @@ def tile_picked_ytenrel_mul_p_kernel(tc, x_words, x_scales, w1, unit, w2, offs, 
         y = [keep.tile([P, S], F32, name=f"y{t}", align_bytes=64) for t in range(4)]
         uy = [keep.tile([P, S], F32, name=f"uy{t}", align_bytes=64) for t in range(4)]
 
-        nc.vector.memset(xs[:].bitcast(I32), 0)
-
         def load_w1(o):
             nc.sync.dma_start(out=w1_raw[o][:], in_=w1[512 * o : 512 * (o + 1), :].rearrange("(p j) c -> p j c", j=4))
 
         def load_x(o):
             nc.sync.dma_start(out=xw[o][:], in_=x_words[o].rearrange("p n r -> p (n r)").bitcast(I32))
 
+        def load_scales():
+            for q in (0, 2, 1, 3):
+                nc.gpsimd.dma_start(out=xs[32 * q : 32 * q + 8, :].bitcast(I32), in_=x_scales[:, 4 * q : 4 * q + 4, :].bitcast(I32))
+
+        nc.gpsimd.memset(xs[:].bitcast(I32), 0)
         nc.sync.dma_start(offs_t[:], offs)
-        load_w1(0)
         load_x(0)
-        for q in range(4):
-            nc.sync.dma_start(out=xs[32 * q : 32 * q + 8, :].bitcast(I32), in_=x_scales[:, 4 * q : 4 * q + 4, :].bitcast(I32))
+        load_scales()
+        nc.gpsimd.dma_start(out=unit_t[:], in_=unit.rearrange("(p t) o -> p (t o)", t=4))
+        load_w1(0)
         load_w1(1)
         load_x(1)
         nc.sync.dma_start(mot_t[:], mot)
+        nc.sync.dma_start(out=w2_raw[:], in_=w2.rearrange("(p j) n -> p j n", j=4))
         nc.sync.dma_start(fat_t[:], fat)
         nc.sync.dma_start(kid_t[:], kid)
-        nc.sync.dma_start(out=unit_t[:], in_=unit.rearrange("(p t) o -> p (t o)", t=4))
-        nc.sync.dma_start(out=w2_raw[:], in_=w2.rearrange("(p j) n -> p j n", j=4))
 
         gw = [keep.tile([P, S], U32, name=f"gw{o}", align_bytes=64) for o in range(2)]
-        gs = keep.tile([P, S], U8, name="gs", align_bytes=64)
         w1_bf = [keep.tile([P, 4 * H], BF16, name=f"w1_bf{o}", align_bytes=64) for o in range(2)]
         w1_c = [keep.tile([P, H], U32, name=f"w1_c{o}", align_bytes=64) for o in range(2)]
         w1_s = [keep.tile([P, H], U8, name=f"w1_s{o}", align_bytes=64) for o in range(2)]
         banks = [psum.tile([P, S], F32, name=f"bank{t}") for t in range(4)]
 
-        def cast_w1(o, copy, m0, m1):
-            dst = w1_bf[o][:].rearrange("p (t m j) -> p m j t", t=4, j=4)[:, m0:m1]
-            src = w1_raw[o][:].rearrange("p j (m t) -> p m j t", t=4)[:, m0:m1]
-            copy(dst, src)
+        def cast_w1(o):
+            dst = w1_bf[o][:].rearrange("p (t m j) -> p m j t", t=4, j=4)
+            src = w1_raw[o][:].rearrange("p j (m t) -> p m j t", t=4)
+            nc.scalar.copy(dst[:, :SCALAR_CAST[o]], src[:, :SCALAR_CAST[o]])
+            nc.vector.tensor_copy(dst[:, SCALAR_CAST[o]:], src[:, SCALAR_CAST[o]:])
 
         def quantize_w1(o):
             nc.vector.quantize_mx(out=w1_c[o][:].bitcast(FP8X4), scales=w1_s[o][:], in_=w1_bf[o][:])
 
-        def gather_x(o):
-            nc.vector.tensor_copy(gw[o][:], xw[o][:].bitcast(U32).indirect(offs_t[:]))
+        def gather_x(o, s0, s1):
+            nc.vector.tensor_copy(gw[o][:, s0:s1], xw[o][:].bitcast(U32).indirect(offs_t[:, s0 // 16 : s1 // 16]))
 
-        def first_product(o):
-            for t in range(4):
-                cols = slice(P * t, P * (t + 1))
-                nc.tensor.matmul_mx(
-                    out=banks[t][:],
-                    lhsT=w1_c[o][:, cols].bitcast(FP8X4),
-                    lhsT_scale=w1_s[o][:, cols],
-                    rhs=gw[o][:].bitcast(FP8X4),
-                    rhs_scale=gs[4 * o : P, :],
-                    start=(o == 0),
-                    stop=(o == 1),
-                )
+        def first_product(o, t, s0, s1):
+            cols = slice(P * t, P * (t + 1))
+            nc.tensor.matmul_mx(
+                out=banks[t][:, s0:s1],
+                lhsT=w1_c[o][:, cols].bitcast(FP8X4),
+                lhsT_scale=w1_s[o][:, cols],
+                rhs=gw[o][:, s0:s1].bitcast(FP8X4),
+                rhs_scale=gs[4 * o : P, s0:s1],
+                start=(o == 0),
+                stop=(o == 1 and s1 == S),
+            )
 
-        cast_w1(0, nc.scalar.copy, 0, 128)
+        gather_x(0, 0, S)
+        gs = keep.tile([P, S], U8, name="gs", tag="xw0", align_bytes=64)
         nc.vector.tensor_copy(gs[:], xs[:].indirect(offs_t[:]))
-        gather_x(0)
+        cast_w1(0)
         quantize_w1(0)
-        first_product(0)
-        cast_w1(1, nc.scalar.copy, 0, 48)
-        cast_w1(1, nc.vector.tensor_copy, 48, 128)
+        cast_w1(1)
         quantize_w1(1)
-        gather_x(1)
-        first_product(1)
+        gather_x(1, 0, S // 2)
+        gather_x(1, S // 2, S)
+        for t in range(4):
+            first_product(0, t, 0, S)
+            first_product(1, t, 0, S // 2)
+            first_product(1, t, S // 2, S)
 
         w2_bf = keep.tile([P, 4 * N], BF16, name="w2_bf", align_bytes=64)
         w2_c = keep.tile([P, N], U32, name="w2_c", align_bytes=64)
         w2_s = keep.tile([P, N], U8, name="w2_s", align_bytes=64)
-
         nc.scalar.copy(w2_bf[:].rearrange("p (c i j) -> p c j i", i=4, j=4), w2_raw[:].rearrange("p j (c i) -> p c j i", i=4))
         nc.vector.quantize_mx(out=w2_c[:].bitcast(FP8X4), scales=w2_s[:], in_=w2_bf[:])
 
@@ -122,7 +126,7 @@ def tile_picked_ytenrel_mul_p_kernel(tc, x_words, x_scales, w1, unit, w2, offs, 
         res = [keep.tile([P, w], F32, name=f"res{c}", align_bytes=64) for c, (w, fused) in enumerate(CHUNKS)]
 
         def leave_bank(t):
-            if t == 1:
+            if t in (1,):
                 nc.vector.tensor_copy(y[t][:], banks[t][:])
             else:
                 nc.scalar.copy(y[t][:], banks[t][:])
@@ -156,15 +160,17 @@ def tile_picked_ytenrel_mul_p_kernel(tc, x_words, x_scales, w1, unit, w2, offs, 
         def second_product(c):
             w = CHUNKS[c][0]
             acc = psum_out.tile([P, 512], F32, name="acc")
-            nc.tensor.matmul_mx(
-                out=acc[:, :w],
-                lhsT=w2_c[:].bitcast(FP8X4),
-                lhsT_scale=w2_s[:],
-                rhs=hid_c[c][:].bitcast(FP8X4),
-                rhs_scale=hid_s[c][:],
-                start=True,
-                stop=True,
-            )
+            for n0 in range(0, w, 256):
+                cols = slice(n0, min(n0 + 256, w))
+                nc.tensor.matmul_mx(
+                    out=acc[:, cols],
+                    lhsT=w2_c[:].bitcast(FP8X4),
+                    lhsT_scale=w2_s[:],
+                    rhs=hid_c[c][:, cols].bitcast(FP8X4),
+                    rhs_scale=hid_s[c][:, cols],
+                    start=True,
+                    stop=True,
+                )
             nc.scalar.copy(res[c][:], acc[:, :w])
             nc.sync.dma_start(out=out[:, starts[c] : starts[c] + w], in_=res[c][:])
 

@@ -17,7 +17,9 @@ P = 128
 K, T, S, H, N, U = 1024, 2048, 512, 512, 128, 1024
 FLOPS = 2 * K * H * S + 2 * H * N * U
 CHUNKS = [(256, True), (384, False), (256, False), (128, False)]
-SCALAR_CAST = (64, 32)
+PARENT_SPANS = [256, 384, 384]
+HALF = S // 2
+SCALAR_CAST = (48, 48)
 
 
 def tile_picked_ytenrel_mul_p_kernel(tc, x_words, x_scales, w1, unit, w2, offs, mot, fat, kid, out):
@@ -25,7 +27,6 @@ def tile_picked_ytenrel_mul_p_kernel(tc, x_words, x_scales, w1, unit, w2, offs, 
     with ExitStack() as ctx:
         keep = ctx.enter_context(tc.tile_pool(name="keep", bufs=1))
         psum = ctx.enter_context(tc.psum_pool(name="psum", bufs=1))
-        psum_out = ctx.enter_context(tc.psum_pool(name="psum_out", bufs=4))
 
         offs_t = keep.tile([P, S // 16], U16, name="offs_t")
         mot_t = keep.tile([P, U // 16], U16, name="mot_t")
@@ -47,30 +48,32 @@ def tile_picked_ytenrel_mul_p_kernel(tc, x_words, x_scales, w1, unit, w2, offs, 
 
         def load_scales():
             for q in (0, 2, 1, 3):
-                nc.gpsimd.dma_start(out=xs[32 * q : 32 * q + 8, :].bitcast(I32), in_=x_scales[:, 4 * q : 4 * q + 4, :].bitcast(I32))
+                nc.sync.dma_start(out=xs[32 * q : 32 * q + 8, :].bitcast(I32), in_=x_scales[:, 4 * q : 4 * q + 4, :].bitcast(I32))
 
-        nc.gpsimd.memset(xs[:].bitcast(I32), 0)
+        nc.vector.memset(xs[:].bitcast(I32), 0)
         nc.sync.dma_start(offs_t[:], offs)
         load_x(0)
         load_scales()
-        nc.gpsimd.dma_start(out=unit_t[:], in_=unit.rearrange("(p t) o -> p (t o)", t=4))
         load_w1(0)
         load_w1(1)
         load_x(1)
         nc.sync.dma_start(mot_t[:], mot)
         nc.sync.dma_start(out=w2_raw[:], in_=w2.rearrange("(p j) n -> p j n", j=4))
         nc.sync.dma_start(fat_t[:], fat)
+        nc.sync.dma_start(out=unit_t[:], in_=unit.rearrange("(p t) o -> p (t o)", t=4))
         nc.sync.dma_start(kid_t[:], kid)
 
-        gw = [keep.tile([P, S], U32, name=f"gw{o}", align_bytes=64) for o in range(2)]
-        w1_bf = [keep.tile([P, 4 * H], BF16, name=f"w1_bf{o}", align_bytes=64) for o in range(2)]
+        gw = [keep.tile([P, S], U32, name=f"gw{o}", tag=f"gw{o}", align_bytes=64) for o in range(2)]
+        w1_bf = {}
         w1_c = [keep.tile([P, H], U32, name=f"w1_c{o}", align_bytes=64) for o in range(2)]
         w1_s = [keep.tile([P, H], U8, name=f"w1_s{o}", align_bytes=64) for o in range(2)]
-        banks = [psum.tile([P, S], F32, name=f"bank{t}") for t in range(4)]
+        pieces = [(t, s0, s1) for t in range(4) for s0, s1 in (((0, HALF), (HALF, S)) if t < 2 else ((0, S),))]
+        banks = {piece: psum.tile([P, 512], F32, name=f"bank{n}", tag=f"bank{n}") for n, piece in enumerate(pieces)}
 
         def cast_w1(o):
-            dst = w1_bf[o][:].rearrange("p (t m j) -> p m j t", t=4, j=4)
-            src = w1_raw[o][:].rearrange("p j (m t) -> p m j t", t=4)
+            w1_bf[o] = keep.tile([P, 4 * H], BF16, name=f"w1_bf{o}", tag="w1_bf", align_bytes=64)
+            dst = w1_bf[o][:].rearrange("p (t m j) -> p m t j", t=4, j=4)
+            src = w1_raw[o][:].rearrange("p j (m t) -> p m t j", t=4)
             nc.scalar.copy(dst[:, :SCALAR_CAST[o]], src[:, :SCALAR_CAST[o]])
             nc.vector.tensor_copy(dst[:, SCALAR_CAST[o]:], src[:, SCALAR_CAST[o]:])
 
@@ -80,16 +83,17 @@ def tile_picked_ytenrel_mul_p_kernel(tc, x_words, x_scales, w1, unit, w2, offs, 
         def gather_x(o, s0, s1):
             nc.vector.tensor_copy(gw[o][:, s0:s1], xw[o][:].bitcast(U32).indirect(offs_t[:, s0 // 16 : s1 // 16]))
 
-        def first_product(o, t, s0, s1):
+        def first_product(o, piece):
+            t, s0, s1 = piece
             cols = slice(P * t, P * (t + 1))
             nc.tensor.matmul_mx(
-                out=banks[t][:, s0:s1],
+                out=banks[piece][:, : s1 - s0],
                 lhsT=w1_c[o][:, cols].bitcast(FP8X4),
                 lhsT_scale=w1_s[o][:, cols],
                 rhs=gw[o][:, s0:s1].bitcast(FP8X4),
                 rhs_scale=gs[4 * o : P, s0:s1],
                 start=(o == 0),
-                stop=(o == 1 and s1 == S),
+                stop=(o == 1),
             )
 
         gather_x(0, 0, S)
@@ -101,50 +105,55 @@ def tile_picked_ytenrel_mul_p_kernel(tc, x_words, x_scales, w1, unit, w2, offs, 
         quantize_w1(1)
         gather_x(1, 0, S // 2)
         gather_x(1, S // 2, S)
-        for t in range(4):
-            first_product(0, t, 0, S)
-            first_product(1, t, 0, S // 2)
-            first_product(1, t, S // 2, S)
+        for piece in pieces:
+            first_product(0, piece)
+        for piece in sorted(pieces, key=lambda piece: (piece[0] // 2, piece[1], piece[0])):
+            first_product(1, piece)
 
-        w2_bf = keep.tile([P, 4 * N], BF16, name="w2_bf", align_bytes=64)
+        w2_bf = keep.tile([P, 4 * N], BF16, name="w2_bf", tag="gw1", align_bytes=64)
         w2_c = keep.tile([P, N], U32, name="w2_c", align_bytes=64)
         w2_s = keep.tile([P, N], U8, name="w2_s", align_bytes=64)
-        nc.scalar.copy(w2_bf[:].rearrange("p (c i j) -> p c j i", i=4, j=4), w2_raw[:].rearrange("p j (c i) -> p c j i", i=4))
-        nc.vector.quantize_mx(out=w2_c[:].bitcast(FP8X4), scales=w2_s[:], in_=w2_bf[:])
 
         starts = [sum(w for w, fused in CHUNKS[:c]) for c in range(len(CHUNKS))]
 
-        def offsets(list_tile, c):
-            return list_tile[:, starts[c] // 16 : (starts[c] + CHUNKS[c][0]) // 16]
+        span_starts = [sum(PARENT_SPANS[:g]) for g in range(len(PARENT_SPANS))]
 
-        mother = [[keep.tile([P, w], F32, name=f"mother{c}_{t}", align_bytes=64) for t in range(4)] for c, (w, fused) in enumerate(CHUNKS)]
-        mid = [keep.tile([P, 4, w], F32, name=f"mid{c}", align_bytes=64) for c, (w, fused) in enumerate(CHUNKS)]
+        def offsets(list_tile, start, width):
+            return list_tile[:, start // 16 : (start + width) // 16]
+
+        def parents(c):
+            g = max(g for g in range(len(PARENT_SPANS)) if span_starts[g] <= starts[c])
+            first = starts[c] - span_starts[g]
+            return mid[g][:, :, first : first + CHUNKS[c][0]]
+
+        mother = [[keep.tile([P, w], F32, name=f"mother{c}_{t}", align_bytes=64) for t in range(4)] for c, w in enumerate(PARENT_SPANS)]
+        mid = [keep.tile([P, 4, w], F32, name=f"mid{c}", align_bytes=64) for c, w in enumerate(PARENT_SPANS)]
         other = [keep.tile([P, 4, w], F32, name=f"other{c}", align_bytes=64) for c, (w, fused) in enumerate(CHUNKS)]
         hid = [keep.tile([P, 4 * w], BF16, name=f"hid{c}", align_bytes=64) for c, (w, fused) in enumerate(CHUNKS)]
         hid_c = [keep.tile([P, w], U32, name=f"hid_c{c}", align_bytes=64) for c, (w, fused) in enumerate(CHUNKS)]
         hid_s = [keep.tile([P, w], U8, name=f"hid_s{c}", align_bytes=64) for c, (w, fused) in enumerate(CHUNKS)]
         res = [keep.tile([P, w], F32, name=f"res{c}", align_bytes=64) for c, (w, fused) in enumerate(CHUNKS)]
 
-        def leave_bank(t):
-            if t in (1,):
-                nc.vector.tensor_copy(y[t][:], banks[t][:])
-            else:
-                nc.scalar.copy(y[t][:], banks[t][:])
+        def leave_banks(t):
+            copy = nc.vector.tensor_copy if t == 1 else nc.scalar.copy
+            for piece in pieces:
+                if piece[0] == t:
+                    copy(y[t][:, piece[1] : piece[2]], banks[piece][:, : piece[2] - piece[1]])
 
         def scale_table(t):
             nc.vector.tensor_scalar_mul(uy[t][:], y[t][:], unit_t[:, t : t + 1])
 
         def gather_mother(c, t):
-            nc.scalar.activation(mother[c][t][:], y[t][:].indirect(offsets(mot_t, c)), COPY)
+            nc.scalar.activation(mother[c][t][:], y[t][:].indirect(offsets(mot_t, span_starts[c], PARENT_SPANS[c])), COPY)
 
         def add_father(c, t):
-            nc.vector.tensor_tensor(mid[c][:, t, :], y[t][:].indirect(offsets(fat_t, c)), mother[c][t][:], ADD)
+            nc.vector.tensor_tensor(mid[c][:, t, :], y[t][:].indirect(offsets(fat_t, span_starts[c], PARENT_SPANS[c])), mother[c][t][:], ADD)
 
         def gather_kid(c, t):
-            nc.scalar.activation(other[c][:, t, :], uy[t][:].indirect(offsets(kid_t, c)), COPY)
+            nc.scalar.activation(other[c][:, t, :], uy[t][:].indirect(offsets(kid_t, starts[c], CHUNKS[c][0])), COPY)
 
         def times_kid(c, t):
-            nc.vector.tensor_tensor(other[c][:, t, :], uy[t][:].indirect(offsets(kid_t, c)), mid[c][:, t, :], MULT)
+            nc.vector.tensor_tensor(other[c][:, t, :], uy[t][:].indirect(offsets(kid_t, starts[c], CHUNKS[c][0])), parents(c)[:, t, :], MULT)
 
         def weave(c):
             dst = hid[c][:].rearrange("p (g i t) -> p g t i", i=4, t=4)
@@ -152,14 +161,14 @@ def tile_picked_ytenrel_mul_p_kernel(tc, x_words, x_scales, w1, unit, w2, offs, 
             if CHUNKS[c][1]:
                 nc.vector.tensor_copy(dst, a)
             else:
-                nc.vector.tensor_tensor(dst, a, mid[c][:].rearrange("p t (g i) -> p g t i", i=4), MULT)
+                nc.vector.tensor_tensor(dst, a, parents(c).rearrange("p t (g i) -> p g t i", i=4), MULT)
 
         def quantize_hid(c):
             nc.vector.quantize_mx(out=hid_c[c][:].bitcast(FP8X4), scales=hid_s[c][:], in_=hid[c][:])
 
         def second_product(c):
             w = CHUNKS[c][0]
-            acc = psum_out.tile([P, 512], F32, name="acc")
+            acc = psum.tile([P, 512], F32, name=f"acc{c}", tag=f"bank{c}")
             for n0 in range(0, w, 256):
                 cols = slice(n0, min(n0 + 256, w))
                 nc.tensor.matmul_mx(
@@ -175,11 +184,12 @@ def tile_picked_ytenrel_mul_p_kernel(tc, x_words, x_scales, w1, unit, w2, offs, 
             nc.sync.dma_start(out=out[:, starts[c] : starts[c] + w], in_=res[c][:])
 
         for t in range(4):
-            leave_bank(t)
+            leave_banks(t)
             gather_mother(0, t)
             scale_table(t)
             add_father(0, t)
-        last = len(CHUNKS) - 1
+        nc.vector.tensor_copy(w2_bf[:].rearrange("p (c i j) -> p c j i", i=4, j=4), w2_raw[:].rearrange("p j (c i) -> p c j i", i=4))
+        last = len(PARENT_SPANS) - 1
         for c in range(len(CHUNKS)):
             for t in range(4):
                 if c < last:
@@ -190,6 +200,8 @@ def tile_picked_ytenrel_mul_p_kernel(tc, x_words, x_scales, w1, unit, w2, offs, 
                     gather_kid(c, t)
                 if c < last and t < 3:
                     add_father(c + 1, t)
+            if c == 0:
+                nc.vector.quantize_mx(out=w2_c[:].bitcast(FP8X4), scales=w2_s[:], in_=w2_bf[:])
             weave(c)
             if c < last:
                 add_father(c + 1, 3)

from contextlib import ExitStack

import concourse.mybir as mybir

F32 = mybir.dt.float32
BF16 = mybir.dt.bfloat16
I32 = mybir.dt.int32
U32 = mybir.dt.uint32
U16 = mybir.dt.uint16
U8 = mybir.dt.uint8
FP8X4 = mybir.dt.float8_e4m3fn_x4
ADD = mybir.AluOpType.add
MULT = mybir.AluOpType.mult
COPY = mybir.ActivationFunctionType.Copy

P = 128
K, T, S, H, N, U = 1024, 2048, 512, 512, 128, 1024
FLOPS = 2 * K * H * S + 2 * H * N * U
CHUNKS = [(256, True), (384, False), (256, False), (128, False)]
PARENT_SPANS = [256, 384, 384]
HALF = S // 2
SCALAR_CAST = (48, 48)


def tile_picked_ytenrel_mul_p_kernel(tc, x_words, x_scales, w1, unit, w2, offs, mot, fat, kid, out):
    nc = tc.nc
    with ExitStack() as ctx:
        keep = ctx.enter_context(tc.tile_pool(name="keep", bufs=1))
        psum = ctx.enter_context(tc.psum_pool(name="psum", bufs=1))

        offs_t = keep.tile([P, S // 16], U16, name="offs_t")
        mot_t = keep.tile([P, U // 16], U16, name="mot_t")
        fat_t = keep.tile([P, U // 16], U16, name="fat_t")
        kid_t = keep.tile([P, U // 16], U16, name="kid_t")
        xw = [keep.tile([P, T], I32, name=f"xw{o}", tag=f"xw{o}", align_bytes=64) for o in range(2)]
        xs = keep.tile([P, T], U8, name="xs", align_bytes=64)
        w1_raw = [keep.tile([P, 4, H], F32, name=f"w1_raw{o}", align_bytes=64) for o in range(2)]
        w2_raw = keep.tile([P, 4, N], F32, name="w2_raw", align_bytes=64)
        unit_t = keep.tile([P, 4], F32, name="unit_t")
        y = [keep.tile([P, S], F32, name=f"y{t}", align_bytes=64) for t in range(4)]
        uy = [keep.tile([P, S], F32, name=f"uy{t}", align_bytes=64) for t in range(4)]

        def load_w1(o):
            nc.sync.dma_start(out=w1_raw[o][:], in_=w1[512 * o : 512 * (o + 1), :].rearrange("(p j) c -> p j c", j=4))

        def load_x(o):
            nc.sync.dma_start(out=xw[o][:], in_=x_words[o].rearrange("p n r -> p (n r)").bitcast(I32))

        def load_scales():
            for q in (0, 2, 1, 3):
                nc.sync.dma_start(out=xs[32 * q : 32 * q + 8, :].bitcast(I32), in_=x_scales[:, 4 * q : 4 * q + 4, :].bitcast(I32))

        nc.vector.memset(xs[:].bitcast(I32), 0)
        nc.sync.dma_start(offs_t[:], offs)
        load_x(0)
        load_scales()
        load_w1(0)
        load_w1(1)
        load_x(1)
        nc.sync.dma_start(mot_t[:], mot)
        nc.sync.dma_start(out=w2_raw[:], in_=w2.rearrange("(p j) n -> p j n", j=4))
        nc.sync.dma_start(fat_t[:], fat)
        nc.sync.dma_start(out=unit_t[:], in_=unit.rearrange("(p t) o -> p (t o)", t=4))
        nc.sync.dma_start(kid_t[:], kid)

        gw = [keep.tile([P, S], U32, name=f"gw{o}", tag=f"gw{o}", align_bytes=64) for o in range(2)]
        w1_bf = {}
        w1_c = [keep.tile([P, H], U32, name=f"w1_c{o}", align_bytes=64) for o in range(2)]
        w1_s = [keep.tile([P, H], U8, name=f"w1_s{o}", align_bytes=64) for o in range(2)]
        pieces = [(t, s0, s1) for t in range(4) for s0, s1 in (((0, HALF), (HALF, S)) if t < 2 else ((0, S),))]
        banks = {piece: psum.tile([P, 512], F32, name=f"bank{n}", tag=f"bank{n}") for n, piece in enumerate(pieces)}

        def cast_w1(o):
            w1_bf[o] = keep.tile([P, 4 * H], BF16, name=f"w1_bf{o}", tag="w1_bf", align_bytes=64)
            dst = w1_bf[o][:].rearrange("p (t m j) -> p m t j", t=4, j=4)
            src = w1_raw[o][:].rearrange("p j (m t) -> p m t j", t=4)
            nc.scalar.copy(dst[:, :SCALAR_CAST[o]], src[:, :SCALAR_CAST[o]])
            nc.vector.tensor_copy(dst[:, SCALAR_CAST[o]:], src[:, SCALAR_CAST[o]:])

        def quantize_w1(o):
            nc.vector.quantize_mx(out=w1_c[o][:].bitcast(FP8X4), scales=w1_s[o][:], in_=w1_bf[o][:])

        def gather_x(o, s0, s1):
            nc.vector.tensor_copy(gw[o][:, s0:s1], xw[o][:].bitcast(U32).indirect(offs_t[:, s0 // 16 : s1 // 16]))

        def first_product(o, piece):
            t, s0, s1 = piece
            cols = slice(P * t, P * (t + 1))
            nc.tensor.matmul_mx(
                out=banks[piece][:, : s1 - s0],
                lhsT=w1_c[o][:, cols].bitcast(FP8X4),
                lhsT_scale=w1_s[o][:, cols],
                rhs=gw[o][:, s0:s1].bitcast(FP8X4),
                rhs_scale=gs[4 * o : P, s0:s1],
                start=(o == 0),
                stop=(o == 1),
            )

        gather_x(0, 0, S)
        gs = keep.tile([P, S], U8, name="gs", tag="xw0", align_bytes=64)
        nc.vector.tensor_copy(gs[:], xs[:].indirect(offs_t[:]))
        cast_w1(0)
        quantize_w1(0)
        cast_w1(1)
        quantize_w1(1)
        gather_x(1, 0, S // 2)
        gather_x(1, S // 2, S)
        for piece in pieces:
            first_product(0, piece)
        for piece in sorted(pieces, key=lambda piece: (piece[0] // 2, piece[1], piece[0])):
            first_product(1, piece)

        w2_bf = keep.tile([P, 4 * N], BF16, name="w2_bf", tag="gw1", align_bytes=64)
        w2_c = keep.tile([P, N], U32, name="w2_c", align_bytes=64)
        w2_s = keep.tile([P, N], U8, name="w2_s", align_bytes=64)

        starts = [sum(w for w, fused in CHUNKS[:c]) for c in range(len(CHUNKS))]

        span_starts = [sum(PARENT_SPANS[:g]) for g in range(len(PARENT_SPANS))]

        def offsets(list_tile, start, width):
            return list_tile[:, start // 16 : (start + width) // 16]

        def parents(c):
            g = max(g for g in range(len(PARENT_SPANS)) if span_starts[g] <= starts[c])
            first = starts[c] - span_starts[g]
            return mid[g][:, :, first : first + CHUNKS[c][0]]

        mother = [[keep.tile([P, w], F32, name=f"mother{c}_{t}", align_bytes=64) for t in range(4)] for c, w in enumerate(PARENT_SPANS)]
        mid = [keep.tile([P, 4, w], F32, name=f"mid{c}", align_bytes=64) for c, w in enumerate(PARENT_SPANS)]
        other = [keep.tile([P, 4, w], F32, name=f"other{c}", align_bytes=64) for c, (w, fused) in enumerate(CHUNKS)]
        hid = [keep.tile([P, 4 * w], BF16, name=f"hid{c}", align_bytes=64) for c, (w, fused) in enumerate(CHUNKS)]
        hid_c = [keep.tile([P, w], U32, name=f"hid_c{c}", align_bytes=64) for c, (w, fused) in enumerate(CHUNKS)]
        hid_s = [keep.tile([P, w], U8, name=f"hid_s{c}", align_bytes=64) for c, (w, fused) in enumerate(CHUNKS)]
        res = [keep.tile([P, w], F32, name=f"res{c}", align_bytes=64) for c, (w, fused) in enumerate(CHUNKS)]

        def leave_banks(t):
            copy = nc.vector.tensor_copy if t == 1 else nc.scalar.copy
            for piece in pieces:
                if piece[0] == t:
                    copy(y[t][:, piece[1] : piece[2]], banks[piece][:, : piece[2] - piece[1]])

        def scale_table(t):
            nc.vector.tensor_scalar_mul(uy[t][:], y[t][:], unit_t[:, t : t + 1])

        def gather_mother(c, t):
            nc.scalar.activation(mother[c][t][:], y[t][:].indirect(offsets(mot_t, span_starts[c], PARENT_SPANS[c])), COPY)

        def add_father(c, t):
            nc.vector.tensor_tensor(mid[c][:, t, :], y[t][:].indirect(offsets(fat_t, span_starts[c], PARENT_SPANS[c])), mother[c][t][:], ADD)

        def gather_kid(c, t):
            nc.scalar.activation(other[c][:, t, :], uy[t][:].indirect(offsets(kid_t, starts[c], CHUNKS[c][0])), COPY)

        def times_kid(c, t):
            nc.vector.tensor_tensor(other[c][:, t, :], uy[t][:].indirect(offsets(kid_t, starts[c], CHUNKS[c][0])), parents(c)[:, t, :], MULT)

        def weave(c):
            dst = hid[c][:].rearrange("p (g i t) -> p g t i", i=4, t=4)
            a = other[c][:].rearrange("p t (g i) -> p g t i", i=4)
            if CHUNKS[c][1]:
                nc.vector.tensor_copy(dst, a)
            else:
                nc.vector.tensor_tensor(dst, a, parents(c).rearrange("p t (g i) -> p g t i", i=4), MULT)

        def quantize_hid(c):
            nc.vector.quantize_mx(out=hid_c[c][:].bitcast(FP8X4), scales=hid_s[c][:], in_=hid[c][:])

        def second_product(c):
            w = CHUNKS[c][0]
            acc = psum.tile([P, 512], F32, name=f"acc{c}", tag=f"bank{c}")
            for n0 in range(0, w, 256):
                cols = slice(n0, min(n0 + 256, w))
                nc.tensor.matmul_mx(
                    out=acc[:, cols],
                    lhsT=w2_c[:].bitcast(FP8X4),
                    lhsT_scale=w2_s[:],
                    rhs=hid_c[c][:, cols].bitcast(FP8X4),
                    rhs_scale=hid_s[c][:, cols],
                    start=True,
                    stop=True,
                )
            nc.scalar.copy(res[c][:], acc[:, :w])
            nc.sync.dma_start(out=out[:, starts[c] : starts[c] + w], in_=res[c][:])

        for t in range(4):
            leave_banks(t)
            gather_mother(0, t)
            scale_table(t)
            add_father(0, t)
        nc.vector.tensor_copy(w2_bf[:].rearrange("p (c i j) -> p c j i", i=4, j=4), w2_raw[:].rearrange("p j (c i) -> p c j i", i=4))
        last = len(PARENT_SPANS) - 1
        for c in range(len(CHUNKS)):
            for t in range(4):
                if c < last:
                    gather_mother(c + 1, t)
                if CHUNKS[c][1]:
                    times_kid(c, t)
                else:
                    gather_kid(c, t)
                if c < last and t < 3:
                    add_father(c + 1, t)
            if c == 0:
                nc.vector.quantize_mx(out=w2_c[:].bitcast(FP8X4), scales=w2_s[:], in_=w2_bf[:])
            weave(c)
            if c < last:
                add_father(c + 1, 3)
            quantize_hid(c)
            second_product(c)
